import numpy as np
import ml_dtypes


def mxq(x, axis, fmt="e4m3"):
    dtype, down = {"e4m3": (ml_dtypes.float8_e4m3fn, 7), "e5m2": (ml_dtypes.float8_e5m2, 14)}[fmt]
    v = np.moveaxis(np.asarray(x, np.float32).astype(ml_dtypes.bfloat16).astype(np.float64), axis, -1)
    blocks = v.reshape(v.shape[:-1] + (-1, 32))
    amax = np.abs(blocks).max(-1, keepdims=True)
    byte = np.maximum(np.where(amax > 0, np.frexp(amax)[1] - 1 + 127, 0) - down, 1)
    scale = np.exp2(byte - 127.0)
    codes = (blocks / scale).astype(np.float32).astype(dtype).astype(np.float64)
    return np.moveaxis((codes * scale).reshape(v.shape), -1, axis)


WIDE = False


def mx_kscale(k):
    if not WIDE:
        return np.ones(k)
    levels = np.array([10, -10, 5, -5, 0])
    if k % 512:
        return np.exp2(np.random.permutation(np.resize(levels, k // 32))).repeat(32)
    a = np.empty((k // 512, 16))
    for p in range(k // 512):
        a[p, :8] = np.random.permutation(np.resize(levels, 8))
        for g in range(8):
            far = levels[np.abs(levels - a[p, g]) >= 10]
            a[p, g + 8] = far[np.random.randint(len(far))]
    return np.exp2(a.ravel()).repeat(32)


def f64(x):
    return np.asarray(x).astype(np.float64)


def striped(idx):
    return np.tile(idx.reshape(-1, 16).T, (8, 1)).astype(np.uint16)


def unstriped(offs):
    return offs[:16].T.reshape(-1).astype(np.int64)


E2M1 = np.array([0.0, 0.5, 1.0, 1.5, 2.0, 3.0, 4.0, 6.0, -0.0, -0.5, -1.0, -1.5, -2.0, -3.0, -4.0, -6.0])


def pack_weight(w, fmt):
    k, n = w.shape
    w = f64(np.asarray(w, np.float32).astype(ml_dtypes.bfloat16)).reshape(k // 32, 32, n)
    amax = np.abs(w).max(1)
    if fmt == "e4m3":
        byte = np.frexp(amax)[1] - 1 + 127 - 7
    else:
        mant, ex = np.frexp(amax / 6.0)
        byte = np.where(mant > 0.5, ex, ex - 1) + 127
    byte = np.clip(np.where(amax > 0, byte, 1), 1, 254)
    scaled = (w * np.exp2(127.0 - byte)[:, None, :]).reshape(k, n).astype(np.float32)
    by_word = np.ascontiguousarray(scaled.reshape(k // 512, 128, 4, n).transpose(0, 1, 3, 2))
    if fmt == "e4m3":
        words = by_word.astype(ml_dtypes.float8_e4m3fn).view(np.uint8)
    else:
        c = by_word.astype(ml_dtypes.float4_e2m1fn).view(np.uint8) & 0xF
        words = (c[..., 0::2] | (c[..., 1::2] << 4)).reshape(k // 512, 128, 2 * n)
    return np.ascontiguousarray(words), np.ascontiguousarray(byte.astype(np.uint8).reshape(k // 512, 16, n))


def unpack_weight(words, scales, fmt):
    g, _, n = scales.shape
    words = np.ascontiguousarray(words).reshape(g, 128, n, -1)
    if fmt == "e4m3":
        vals = words.view(ml_dtypes.float8_e4m3fn).astype(np.float64)
    else:
        nib = np.empty((g, 128, n, 4), np.uint8)
        nib[..., 0::2] = words & 0xF
        nib[..., 1::2] = words >> 4
        vals = E2M1[nib]
    vals = vals * np.repeat(np.exp2(scales.astype(np.float64) - 127.0), 8, axis=1)[..., None]
    return vals.transpose(0, 1, 3, 2).reshape(g * 512, n)


def pack_table(v):
    words, scales = pack_weight(v, "e4m3")
    return np.concatenate([words.reshape(words.shape[0], -1), scales.reshape(scales.shape[0], -1)], axis=1)


def unpack_table(tab):
    g, t = tab.shape[0], tab.shape[1] // 528
    return unpack_weight(tab[:, :512 * t].reshape(g, 128, t, 4), tab[:, 512 * t:].reshape(g, 16, t), "e4m3")


def silu(v):
    return v / (1.0 + np.exp(-np.maximum(v, -700.0)))


K, M, T, S = 512, 512, 1024, 512


def setup_inputs():
    n = np.random.standard_normal
    s = mx_kscale(K)[:, None]
    p_w4 = pack_weight(n((K, M)) / np.sqrt(K) / s, "e2m1")
    return {
        "tab": pack_table(n((K, T)) * s),
        "w4_words": p_w4[0],
        "w4_scales": p_w4[1],
        "w8": (n((K, M)) / np.sqrt(K) / s).astype(np.float32),
        "r": (n((512, 512))).astype(np.float32),
        "offs": striped(np.random.permutation(T)[:S]),
    }


def reference(tab, w4_words, w4_scales, w8, r, offs):
    tab_ = unpack_table(tab)[:, unstriped(offs)]
    w4_ = unpack_weight(w4_words, w4_scales, "e2m1")
    w8_ = mxq(f64(w8), 0, "e4m3")
    y = w4_.T @ tab_
    u = w8_.T @ tab_
    y = silu(y) * u
    return f64(r) + y

@@ -1,0 +1,173 @@
+import concourse.mybir as mybir
+
+F32 = mybir.dt.float32
+BF16 = mybir.dt.bfloat16
+I32 = mybir.dt.int32
+U32 = mybir.dt.uint32
+U16 = mybir.dt.uint16
+U8 = mybir.dt.uint8
+FP8X4 = mybir.dt.float8_e4m3fn_x4
+FP4X4 = mybir.dt.float4_e2m1fn_x4
+SILU = mybir.ActivationFunctionType.Silu
+MULT = mybir.AluOpType.mult
+ADD = mybir.AluOpType.add
+
+P = 128
+T = 1024
+S = 512
+N = 512
+NT = N // P
+FLOPS = 2 * 2 * 512 * N * S
+
+
+def tile_list_tabglu_res_kernel(tc, tab, w4_words, w4_scales, w8, r, offs, out):
+    nc = tc.nc
+    with (
+        tc.tile_pool(name="held", bufs=1) as held,
+        tc.psum_pool(name="psum", bufs=1) as psum,
+    ):
+        offs_t = held.tile([P, S // 16], U16, name="offs_t")
+        tab_s = held.tile([P, T // 4], I32, name="tab_s", align_bytes=64)
+        tab_w = held.tile([P, T], I32, name="tab_w", align_bytes=64)
+        w4_s = held.tile([P, N], U8, name="w4_s", align_bytes=64)
+        w4_w = held.tile([P, 2 * N], U8, name="w4_w", align_bytes=64)
+        x_w = held.tile([P, S], U32, name="x_w", align_bytes=64)
+        x_s = held.tile([P, S], U8, name="x_s", align_bytes=64)
+        w8_c = held.tile([P, N], U32, name="w8_c", align_bytes=64)
+        w8_s = held.tile([P, N], U8, name="w8_s", align_bytes=64)
+        warm = held.tile([P, 1], F32, name="warm")
+
+        nc.gpsimd.memset(tab_s[:], 0)
+        nc.gpsimd.memset(w4_s[:].bitcast(I32), 0)
+        nc.vector.memset(warm[:], 0.0)
+        scale_rows = tab[0, 512 * T : 528 * T].bitcast(I32).rearrange("(q s t) -> s q t", q=4, s=4)
+        w4_rows = w4_scales[0].bitcast(I32).rearrange("(q s) n -> s q n", q=4, s=4)
+        nc.sync.dma_start(offs_t[:], offs)
+        for s in range(4):
+            nc.scalar.dma_start(out=tab_s[s:P:32, :], in_=scale_rows[s])
+        nc.scalar.activation(out=warm[:], in_=warm[:], func=SILU)
+        nc.sync.dma_start(out=tab_w[:], in_=tab[0, 0 : 512 * T].bitcast(I32).rearrange("(p t) -> p t", p=P))
+        w8_v = w8.rearrange("(p j) n -> p j n", j=4)
+        raws = []
+        for h in range(2):
+            raw = held.tile([P, 4, 256], F32, name=f"raw{h}")
+            nc.sync.dma_start(out=raw[:], in_=w8_v[:, :, 256 * h : 256 * h + 256])
+            raws.append(raw)
+        nc.scalar.dma_start(out=w4_w[:].bitcast(I32), in_=w4_words[0].bitcast(I32))
+        for s in range(4):
+            nc.scalar.dma_start(out=w4_s[s:P:32, :].bitcast(I32), in_=w4_rows[s])
+        rts = []
+        for h in range(2):
+            rt = held.tile([P, 2, S], F32, name=f"r{h}")
+            nc.sync.dma_start(out=rt[:], in_=r[2 * P * h : 2 * P * h + 2 * P, :].rearrange("(a p) s -> p a s", p=P))
+            rts += [rt[:, 0, :], rt[:, 1, :]]
+
+        nc.vector.tensor_copy(out=x_s[:], in_=tab_s[:].bitcast(U8).indirect(offs_t[:]))
+        for h in range(2):
+            nc.vector.tensor_copy(
+                out=x_w[:, 256 * h : 256 * h + 256], in_=tab_w[:].bitcast(U32).indirect(offs_t[:, 16 * h : 16 * h + 16])
+            )
+
+        groups = []
+        for i in range(NT):
+            g = held.tile([P, P, 4], BF16, name=f"g{i}", align_bytes=64)
+            groups.append(g)
+        es = []
+        us = []
+        for i in range(NT):
+            e = psum.tile([P, S], F32, name=f"e{i}")
+            es.append(e)
+            u = psum.tile([P, S], F32, name=f"u{i}")
+            us.append(u)
+
+        def inter(i):
+            src = raws[i // 2][:, :, P * (i % 2) : P * (i % 2) + P].rearrange("p j n -> p n j")
+            if i % 2 == 0:
+                nc.scalar.copy(out=groups[i][:], in_=src)
+            else:
+                nc.vector.tensor_copy(out=groups[i][:], in_=src)
+
+        def quant(i):
+            c = slice(P * i, P * i + P)
+            nc.vector.quantize_mx(out=w8_c[:, c].bitcast(FP8X4), scales=w8_s[:, c], in_=groups[i][:].rearrange("p n j -> p (n j)"))
+
+        def gate(i):
+            c = slice(P * i, P * i + P)
+            for h in range(2):
+                d = slice(256 * h, 256 * h + 256)
+                nc.tensor.matmul_mx(
+                    out=es[i][:, d],
+                    lhsT=w4_w[:, 2 * P * i : 2 * P * i + 2 * P].bitcast(FP4X4),
+                    lhsT_scale=w4_s[:, c],
+                    rhs=x_w[:, d].bitcast(FP8X4),
+                    rhs_scale=x_s[:, d],
+                    start=True,
+                    stop=True,
+                )
+
+        def up(i):
+            c = slice(P * i, P * i + P)
+            for h in range(2):
+                d = slice(256 * h, 256 * h + 256)
+                nc.tensor.matmul_mx(
+                    out=us[i][:, d],
+                    lhsT=w8_c[:, c].bitcast(FP8X4),
+                    lhsT_scale=w8_s[:, c],
+                    rhs=x_w[:, d].bitcast(FP8X4),
+                    rhs_scale=x_s[:, d],
+                    start=True,
+                    stop=True,
+                )
+
+        sils = []
+        for i in range(NT):
+            sil = held.tile([P, S], F32, name=f"sil{i}")
+            sils.append(sil)
+        ys = []
+        for i in range(NT):
+            y = held.tile([P, S], F32, name=f"y{i}")
+            ys.append(y)
+        ots = []
+        for i in range(NT):
+            o = held.tile([P, S], F32, name=f"o{i}")
+            ots.append(o)
+
+        def silu(i, parts=1):
+            for k in range(parts):
+                d = slice(S // parts * k, S // parts * k + S // parts)
+                nc.scalar.activation(out=sils[i][:, d], in_=es[i][:, d], func=SILU)
+
+        def mul(i, parts=1):
+            for k in range(parts):
+                d = slice(S // parts * k, S // parts * k + S // parts)
+                nc.vector.tensor_tensor(out=ys[i][:, d], in0=us[i][:, d], in1=sils[i][:, d], op=MULT)
+
+        def add(i):
+            parts = ((nc.gpsimd, 0, S),) if i == 0 else ((nc.gpsimd, 0, 192), (nc.vector, 192, S)) if i == 1 else ((nc.vector, 0, S),)
+            for eng, a, b in parts:
+                eng.tensor_tensor(out=ots[i][:, a:b], in0=ys[i][:, a:b], in1=rts[i][:, a:b], op=ADD)
+            nc.sync.dma_start(out=out[P * i : P * i + P, :], in_=ots[i][:])
+
+        inter(0)
+        inter(1)
+        quant(0)
+        inter(2)
+        quant(1)
+        inter(3)
+        quant(2)
+        quant(3)
+        for i in range(NT):
+            gate(i)
+            up(i)
+        silu(0)
+        mul(0, 2)
+        add(0)
+        silu(1)
+        mul(1)
+        silu(2)
+        mul(2)
+        silu(3)
+        mul(3)
+        add(1)
+        add(2)
+        add(3)

@@ -39,12 +39,12 @@ def tile_list_tabglu_res_kernel(tc, tab, w4_words, w4_scales, w8, r, offs, out):
 
         nc.gpsimd.memset(tab_s[:], 0)
         nc.gpsimd.memset(w4_s[:].bitcast(I32), 0)
-        nc.vector.memset(warm[:], 0.0)
+        nc.gpsimd.memset(warm[:], 0.0)
         scale_rows = tab[0, 512 * T : 528 * T].bitcast(I32).rearrange("(q s t) -> s q t", q=4, s=4)
         w4_rows = w4_scales[0].bitcast(I32).rearrange("(q s) n -> s q n", q=4, s=4)
         nc.sync.dma_start(offs_t[:], offs)
         for s in range(4):
-            nc.scalar.dma_start(out=tab_s[s:P:32, :], in_=scale_rows[s])
+            nc.sync.dma_start(out=tab_s[s:P:32, :], in_=scale_rows[s])
         nc.scalar.activation(out=warm[:], in_=warm[:], func=SILU)
         nc.sync.dma_start(out=tab_w[:], in_=tab[0, 0 : 512 * T].bitcast(I32).rearrange("(p t) -> p t", p=P))
         w8_v = w8.rearrange("(p j) n -> p j n", j=4)
@@ -151,22 +151,27 @@ def tile_list_tabglu_res_kernel(tc, tab, w4_words, w4_scales, w8, r, offs, out):
         inter(0)
         inter(1)
         quant(0)
-        inter(2)
         quant(1)
-        inter(3)
-        quant(2)
-        quant(3)
-        for i in range(NT):
-            gate(i)
-            up(i)
+        gate(0)
+        gate(1)
+        up(0)
+        gate(2)
         silu(0)
-        mul(0, 2)
-        add(0)
         silu(1)
+        inter(3)
+        inter(2)
+        quant(3)
+        up(1)
+        gate(3)
+        mul(0)
+        add(0)
         mul(1)
         silu(2)
-        mul(2)
+        quant(2)
+        up(2)
+        up(3)
         silu(3)
+        mul(2)
         mul(3)
         add(1)
         add(2)

@@ -53,9 +53,10 @@ def tile_list_tabglu_res_kernel(tc, tab, w4_words, w4_scales, w8, r, offs, out):
             raw = held.tile([P, 4, 256], F32, name=f"raw{h}")
             nc.sync.dma_start(out=raw[:], in_=w8_v[:, :, 256 * h : 256 * h + 256])
             raws.append(raw)
-        nc.scalar.dma_start(out=w4_w[:].bitcast(I32), in_=w4_words[0].bitcast(I32))
-        for s in range(4):
-            nc.scalar.dma_start(out=w4_s[s:P:32, :].bitcast(I32), in_=w4_rows[s])
+            if h == 0:
+                nc.sync.dma_start(out=w4_w[:].bitcast(I32), in_=w4_words[0].bitcast(I32))
+                for s in range(4):
+                    nc.sync.dma_start(out=w4_s[s:P:32, :].bitcast(I32), in_=w4_rows[s])
         rts = []
         for h in range(2):
             rt = held.tile([P, 2, S], F32, name=f"r{h}")
@@ -75,17 +76,12 @@ def tile_list_tabglu_res_kernel(tc, tab, w4_words, w4_scales, w8, r, offs, out):
         es = []
         us = []
         for i in range(NT):
-            e = psum.tile([P, S], F32, name=f"e{i}")
+            e = psum.tile([P, S], F32, name=f"e{i}", tag=f"bank{i}")
             es.append(e)
-            u = psum.tile([P, S], F32, name=f"u{i}")
-            us.append(u)
 
         def inter(i):
             src = raws[i // 2][:, :, P * (i % 2) : P * (i % 2) + P].rearrange("p j n -> p n j")
-            if i % 2 == 0:
-                nc.scalar.copy(out=groups[i][:], in_=src)
-            else:
-                nc.vector.tensor_copy(out=groups[i][:], in_=src)
+            nc.vector.tensor_copy(out=groups[i][:], in_=src)
 
         def quant(i):
             c = slice(P * i, P * i + P)
@@ -143,7 +139,7 @@ def tile_list_tabglu_res_kernel(tc, tab, w4_words, w4_scales, w8, r, offs, out):
                 nc.vector.tensor_tensor(out=ys[i][:, d], in0=us[i][:, d], in1=sils[i][:, d], op=MULT)
 
         def add(i):
-            parts = ((nc.gpsimd, 0, S),) if i == 0 else ((nc.gpsimd, 0, 192), (nc.vector, 192, S)) if i == 1 else ((nc.vector, 0, S),)
+            parts = ((nc.gpsimd if i < 2 else nc.vector, 0, S),)
             for eng, a, b in parts:
                 eng.tensor_tensor(out=ots[i][:, a:b], in0=ys[i][:, a:b], in1=rts[i][:, a:b], op=ADD)
             nc.sync.dma_start(out=out[P * i : P * i + P, :], in_=ots[i][:])
@@ -152,27 +148,19 @@ def tile_list_tabglu_res_kernel(tc, tab, w4_words, w4_scales, w8, r, offs, out):
         inter(1)
         quant(0)
         quant(1)
-        gate(0)
-        gate(1)
-        up(0)
-        gate(2)
-        silu(0)
-        silu(1)
-        inter(3)
         inter(2)
-        quant(3)
-        up(1)
-        gate(3)
-        mul(0)
-        add(0)
-        mul(1)
-        silu(2)
+        inter(3)
         quant(2)
-        up(2)
-        up(3)
-        silu(3)
-        mul(2)
-        mul(3)
-        add(1)
-        add(2)
-        add(3)
+        quant(3)
+        for i in range(NT):
+            gate(i)
+        for i in range(NT):
+            silu(i)
+        for i in range(NT):
+            u = psum.tile([P, S], F32, name=f"u{i}", tag=f"bank{i}")
+            us.append(u)
+            up(i)
+        for i in range(NT):
+            mul(i)
+        for i in range(NT):
+            add(i)

@@ -64,103 +64,70 @@ def tile_list_tabglu_res_kernel(tc, tab, w4_words, w4_scales, w8, r, offs, out):
             rts += [rt[:, 0, :], rt[:, 1, :]]
 
         nc.vector.tensor_copy(out=x_s[:], in_=tab_s[:].bitcast(U8).indirect(offs_t[:]))
-        for h in range(2):
-            nc.vector.tensor_copy(
-                out=x_w[:, 256 * h : 256 * h + 256], in_=tab_w[:].bitcast(U32).indirect(offs_t[:, 16 * h : 16 * h + 16])
-            )
+        nc.vector.tensor_copy(out=x_w[:], in_=tab_w[:].bitcast(U32).indirect(offs_t[:]))
 
-        groups = []
-        for i in range(NT):
-            g = held.tile([P, P, 4], BF16, name=f"g{i}", align_bytes=64)
-            groups.append(g)
+        for h in range(2):
+            g = held.tile([P, 256, 4], BF16, name=f"g{h}", align_bytes=64)
+            nc.vector.tensor_copy(out=g[:], in_=raws[h][:].rearrange("p j n -> p n j"))
+            c = slice(256 * h, 256 * h + 256)
+            nc.vector.quantize_mx(out=w8_c[:, c].bitcast(FP8X4), scales=w8_s[:, c], in_=g[:].rearrange("p n j -> p (n j)"))
+
         es = []
         us = []
-        for i in range(NT):
-            e = psum.tile([P, S], F32, name=f"e{i}", tag=f"bank{i}")
-            es.append(e)
-
-        def inter(i):
-            src = raws[i // 2][:, :, P * (i % 2) : P * (i % 2) + P].rearrange("p j n -> p n j")
-            nc.vector.tensor_copy(out=groups[i][:], in_=src)
-
-        def quant(i):
-            c = slice(P * i, P * i + P)
-            nc.vector.quantize_mx(out=w8_c[:, c].bitcast(FP8X4), scales=w8_s[:, c], in_=groups[i][:].rearrange("p n j -> p (n j)"))
+        sils = []
 
         def gate(i):
-            c = slice(P * i, P * i + P)
-            for h in range(2):
-                d = slice(256 * h, 256 * h + 256)
+            parts = 2 if i < 2 else 1
+            w = S // parts
+            es.append([psum.tile([P, w], F32, name=f"e{i}_{k}", tag=f"bank{i + 2 * k}") for k in range(parts)])
+            for k, e in enumerate(es[i]):
+                d = slice(w * k, w * k + w)
                 nc.tensor.matmul_mx(
-                    out=es[i][:, d],
+                    out=e[:],
                     lhsT=w4_w[:, 2 * P * i : 2 * P * i + 2 * P].bitcast(FP4X4),
-                    lhsT_scale=w4_s[:, c],
+                    lhsT_scale=w4_s[:, P * i : P * i + P],
                     rhs=x_w[:, d].bitcast(FP8X4),
                     rhs_scale=x_s[:, d],
                     start=True,
                     stop=True,
                 )
 
-        def up(i):
-            c = slice(P * i, P * i + P)
-            for h in range(2):
-                d = slice(256 * h, 256 * h + 256)
-                nc.tensor.matmul_mx(
-                    out=us[i][:, d],
-                    lhsT=w8_c[:, c].bitcast(FP8X4),
-                    lhsT_scale=w8_s[:, c],
-                    rhs=x_w[:, d].bitcast(FP8X4),
-                    rhs_scale=x_s[:, d],
-                    start=True,
-                    stop=True,
-                )
-
-        sils = []
-        for i in range(NT):
+        def silu(i):
             sil = held.tile([P, S], F32, name=f"sil{i}")
             sils.append(sil)
-        ys = []
-        for i in range(NT):
-            y = held.tile([P, S], F32, name=f"y{i}")
-            ys.append(y)
-        ots = []
-        for i in range(NT):
-            o = held.tile([P, S], F32, name=f"o{i}")
-            ots.append(o)
+            w = S // len(es[i])
+            for k, e in enumerate(es[i]):
+                nc.scalar.activation(out=sil[:, w * k : w * k + w], in_=e[:], func=SILU)
 
-        def silu(i, parts=1):
-            for k in range(parts):
-                d = slice(S // parts * k, S // parts * k + S // parts)
-                nc.scalar.activation(out=sils[i][:, d], in_=es[i][:, d], func=SILU)
-
-        def mul(i, parts=1):
-            for k in range(parts):
-                d = slice(S // parts * k, S // parts * k + S // parts)
-                nc.vector.tensor_tensor(out=ys[i][:, d], in0=us[i][:, d], in1=sils[i][:, d], op=MULT)
-
-        def add(i):
-            parts = ((nc.gpsimd if i < 2 else nc.vector, 0, S),)
-            for eng, a, b in parts:
-                eng.tensor_tensor(out=ots[i][:, a:b], in0=ys[i][:, a:b], in1=rts[i][:, a:b], op=ADD)
-            nc.sync.dma_start(out=out[P * i : P * i + P, :], in_=ots[i][:])
-
-        inter(0)
-        inter(1)
-        quant(0)
-        quant(1)
-        inter(2)
-        inter(3)
-        quant(2)
-        quant(3)
-        for i in range(NT):
-            gate(i)
-        for i in range(NT):
-            silu(i)
-        for i in range(NT):
+        def up(i):
             u = psum.tile([P, S], F32, name=f"u{i}", tag=f"bank{i}")
             us.append(u)
+            c = slice(P * i, P * i + P)
+            nc.tensor.matmul_mx(
+                out=u[:],
+                lhsT=w8_c[:, c].bitcast(FP8X4),
+                lhsT_scale=w8_s[:, c],
+                rhs=x_w[:].bitcast(FP8X4),
+                rhs_scale=x_s[:],
+                start=True,
+                stop=True,
+            )
+
+        gate(0)
+        gate(1)
+        silu(0)
+        silu(1)
+        for i in range(NT):
+            if i >= 2:
+                gate(i)
+                silu(i)
             up(i)
         for i in range(NT):
-            mul(i)
-        for i in range(NT):
-            add(i)
+            y = held.tile([P, S], F32, name=f"y{i}")
+            nc.vector.tensor_tensor(out=y[:], in0=us[i][:], in1=sils[i][:], op=MULT)
+            o = held.tile([P, S], F32, name=f"o{i}")
+            eng, queue = (nc.gpsimd, nc.scalar) if i < 2 else (nc.vector, nc.sync)
+            for k in range(2):
+                d = slice(256 * k, 256 * k + 256)
+                eng.tensor_tensor(out=o[:, d], in0=y[:, d], in1=rts[i][:, d], op=ADD)
+                queue.dma_start(out=out[P * i : P * i + P, d], in_=o[:, d])

@@ -64,7 +64,10 @@ def tile_list_tabglu_res_kernel(tc, tab, w4_words, w4_scales, w8, r, offs, out):
             rts += [rt[:, 0, :], rt[:, 1, :]]
 
         nc.vector.tensor_copy(out=x_s[:], in_=tab_s[:].bitcast(U8).indirect(offs_t[:]))
-        nc.vector.tensor_copy(out=x_w[:], in_=tab_w[:].bitcast(U32).indirect(offs_t[:]))
+        for h in range(2):
+            nc.vector.tensor_copy(
+                out=x_w[:, 256 * h : 256 * h + 256], in_=tab_w[:].bitcast(U32).indirect(offs_t[:, 16 * h : 16 * h + 16])
+            )
 
         for h in range(2):
             g = held.tile([P, 256, 4], BF16, name=f"g{h}", align_bytes=64)
@@ -72,35 +75,26 @@ def tile_list_tabglu_res_kernel(tc, tab, w4_words, w4_scales, w8, r, offs, out):
             c = slice(256 * h, 256 * h + 256)
             nc.vector.quantize_mx(out=w8_c[:, c].bitcast(FP8X4), scales=w8_s[:, c], in_=g[:].rearrange("p n j -> p (n j)"))
 
-        es = []
-        us = []
+        def gate(i, h, e):
+            d = slice(256 * h, 256 * h + 256)
+            nc.tensor.matmul_mx(
+                out=e,
+                lhsT=w4_w[:, 2 * P * i : 2 * P * i + 2 * P].bitcast(FP4X4),
+                lhsT_scale=w4_s[:, P * i : P * i + P],
+                rhs=x_w[:, d].bitcast(FP8X4),
+                rhs_scale=x_s[:, d],
+                start=True,
+                stop=True,
+            )
+
         sils = []
-
-        def gate(i):
-            parts = 2 if i < 2 else 1
-            w = S // parts
-            es.append([psum.tile([P, w], F32, name=f"e{i}_{k}", tag=f"bank{i + 2 * k}") for k in range(parts)])
-            for k, e in enumerate(es[i]):
-                d = slice(w * k, w * k + w)
-                nc.tensor.matmul_mx(
-                    out=e[:],
-                    lhsT=w4_w[:, 2 * P * i : 2 * P * i + 2 * P].bitcast(FP4X4),
-                    lhsT_scale=w4_s[:, P * i : P * i + P],
-                    rhs=x_w[:, d].bitcast(FP8X4),
-                    rhs_scale=x_s[:, d],
-                    start=True,
-                    stop=True,
-                )
-
-        def silu(i):
+        for i in range(NT):
             sil = held.tile([P, S], F32, name=f"sil{i}")
             sils.append(sil)
-            w = S // len(es[i])
-            for k, e in enumerate(es[i]):
-                nc.scalar.activation(out=sil[:, w * k : w * k + w], in_=e[:], func=SILU)
+        us = []
 
-        def up(i):
-            u = psum.tile([P, S], F32, name=f"u{i}", tag=f"bank{i}")
+        def up(i, bank):
+            u = psum.tile([P, S], F32, name=f"u{i}", tag=bank)
             us.append(u)
             c = slice(P * i, P * i + P)
             nc.tensor.matmul_mx(
@@ -113,21 +107,37 @@ def tile_list_tabglu_res_kernel(tc, tab, w4_words, w4_scales, w8, r, offs, out):
                 stop=True,
             )
 
-        gate(0)
-        gate(1)
-        silu(0)
-        silu(1)
-        for i in range(NT):
-            if i >= 2:
-                gate(i)
-                silu(i)
-            up(i)
+        e00 = psum.tile([P, 256], F32, name="e00", tag="bank0")
+        e01 = psum.tile([P, 256], F32, name="e01", tag="bank1")
+        e10 = psum.tile([P, 256], F32, name="e10", tag="bank2")
+        e11 = psum.tile([P, 256], F32, name="e11", tag="bank3")
+        e2 = psum.tile([P, S], F32, name="e2", tag="bank4")
+        gate(0, 0, e00[:])
+        gate(1, 0, e10[:])
+        gate(2, 0, e2[:, 0:256])
+        gate(0, 1, e01[:])
+        gate(1, 1, e11[:])
+        gate(2, 1, e2[:, 256:512])
+        nc.scalar.activation(out=sils[0][:, 0:256], in_=e00[:], func=SILU)
+        nc.scalar.activation(out=sils[1][:, 0:256], in_=e10[:], func=SILU)
+        nc.scalar.activation(out=sils[0][:, 256:512], in_=e01[:], func=SILU)
+        nc.scalar.activation(out=sils[1][:, 256:512], in_=e11[:], func=SILU)
+        nc.scalar.activation(out=sils[2][:], in_=e2[:], func=SILU)
+        up(0, "bank0")
+        up(1, "bank1")
+        up(2, "bank2")
+        e3 = psum.tile([P, S], F32, name="e3", tag="bank3")
+        gate(3, 0, e3[:, 0:256])
+        gate(3, 1, e3[:, 256:512])
+        nc.scalar.activation(out=sils[3][:], in_=e3[:], func=SILU)
+        up(3, "bank4")
         for i in range(NT):
             y = held.tile([P, S], F32, name=f"y{i}")
             nc.vector.tensor_tensor(out=y[:], in0=us[i][:], in1=sils[i][:], op=MULT)
             o = held.tile([P, S], F32, name=f"o{i}")
             eng, queue = (nc.gpsimd, nc.scalar) if i < 2 else (nc.vector, nc.sync)
-            for k in range(2):
-                d = slice(256 * k, 256 * k + 256)
+            parts = 2 if i == NT - 1 else 1
+            for k in range(parts):
+                d = slice(S // parts * k, S // parts * k + S // parts)
                 eng.tensor_tensor(out=o[:, d], in0=y[:, d], in1=rts[i][:, d], op=ADD)
                 queue.dma_start(out=out[P * i : P * i + P, d], in_=o[:, d])

import concourse.mybir as mybir

F32 = mybir.dt.float32
BF16 = mybir.dt.bfloat16
I32 = mybir.dt.int32
U32 = mybir.dt.uint32
U16 = mybir.dt.uint16
U8 = mybir.dt.uint8
FP8X4 = mybir.dt.float8_e4m3fn_x4
FP4X4 = mybir.dt.float4_e2m1fn_x4
SILU = mybir.ActivationFunctionType.Silu
MULT = mybir.AluOpType.mult
ADD = mybir.AluOpType.add

P = 128
T = 1024
S = 512
N = 512
NT = N // P
FLOPS = 2 * 2 * 512 * N * S


def tile_list_tabglu_res_kernel(tc, tab, w4_words, w4_scales, w8, r, offs, out):
    nc = tc.nc
    with (
        tc.tile_pool(name="held", bufs=1) as held,
        tc.psum_pool(name="psum", bufs=1) as psum,
    ):
        offs_t = held.tile([P, S // 16], U16, name="offs_t")
        tab_s = held.tile([P, T // 4], I32, name="tab_s", align_bytes=64)
        tab_w = held.tile([P, T], I32, name="tab_w", align_bytes=64)
        w4_s = held.tile([P, N], U8, name="w4_s", align_bytes=64)
        w4_w = held.tile([P, 2 * N], U8, name="w4_w", align_bytes=64)
        x_w = held.tile([P, S], U32, name="x_w", align_bytes=64)
        x_s = held.tile([P, S], U8, name="x_s", align_bytes=64)
        w8_c = held.tile([P, N], U32, name="w8_c", align_bytes=64)
        w8_s = held.tile([P, N], U8, name="w8_s", align_bytes=64)
        warm = held.tile([P, 1], F32, name="warm")

        nc.gpsimd.memset(tab_s[:], 0)
        nc.gpsimd.memset(w4_s[:].bitcast(I32), 0)
        nc.gpsimd.memset(warm[:], 0.0)
        scale_rows = tab[0, 512 * T : 528 * T].bitcast(I32).rearrange("(q s t) -> s q t", q=4, s=4)
        w4_rows = w4_scales[0].bitcast(I32).rearrange("(q s) n -> s q n", q=4, s=4)
        nc.sync.dma_start(offs_t[:], offs)
        for s in range(4):
            nc.sync.dma_start(out=tab_s[s:P:32, :], in_=scale_rows[s])
        nc.scalar.activation(out=warm[:], in_=warm[:], func=SILU)
        nc.sync.dma_start(out=tab_w[:], in_=tab[0, 0 : 512 * T].bitcast(I32).rearrange("(p t) -> p t", p=P))
        w8_v = w8.rearrange("(p j) n -> p j n", j=4)
        raws = []
        for h in range(2):
            raw = held.tile([P, 4, 256], F32, name=f"raw{h}")
            nc.sync.dma_start(out=raw[:], in_=w8_v[:, :, 256 * h : 256 * h + 256])
            raws.append(raw)
            if h == 0:
                nc.sync.dma_start(out=w4_w[:].bitcast(I32), in_=w4_words[0].bitcast(I32))
                for s in range(4):
                    nc.sync.dma_start(out=w4_s[s:P:32, :].bitcast(I32), in_=w4_rows[s])
        rts = []
        for h in range(2):
            rt = held.tile([P, 2, S], F32, name=f"r{h}")
            nc.sync.dma_start(out=rt[:], in_=r[2 * P * h : 2 * P * h + 2 * P, :].rearrange("(a p) s -> p a s", p=P))
            rts += [rt[:, 0, :], rt[:, 1, :]]

        nc.vector.tensor_copy(out=x_s[:], in_=tab_s[:].bitcast(U8).indirect(offs_t[:]))
        for h in range(2):
            nc.vector.tensor_copy(
                out=x_w[:, 256 * h : 256 * h + 256], in_=tab_w[:].bitcast(U32).indirect(offs_t[:, 16 * h : 16 * h + 16])
            )

        for h in range(2):
            g = held.tile([P, 256, 4], BF16, name=f"g{h}", align_bytes=64)
            nc.vector.tensor_copy(out=g[:], in_=raws[h][:].rearrange("p j n -> p n j"))
            c = slice(256 * h, 256 * h + 256)
            nc.vector.quantize_mx(out=w8_c[:, c].bitcast(FP8X4), scales=w8_s[:, c], in_=g[:].rearrange("p n j -> p (n j)"))

        def gate(i, h, e):
            d = slice(256 * h, 256 * h + 256)
            nc.tensor.matmul_mx(
                out=e,
                lhsT=w4_w[:, 2 * P * i : 2 * P * i + 2 * P].bitcast(FP4X4),
                lhsT_scale=w4_s[:, P * i : P * i + P],
                rhs=x_w[:, d].bitcast(FP8X4),
                rhs_scale=x_s[:, d],
                start=True,
                stop=True,
            )

        sils = []
        for i in range(NT):
            sil = held.tile([P, S], F32, name=f"sil{i}")
            sils.append(sil)
        us = []

        def up(i, bank):
            u = psum.tile([P, S], F32, name=f"u{i}", tag=bank)
            us.append(u)
            c = slice(P * i, P * i + P)
            nc.tensor.matmul_mx(
                out=u[:],
                lhsT=w8_c[:, c].bitcast(FP8X4),
                lhsT_scale=w8_s[:, c],
                rhs=x_w[:].bitcast(FP8X4),
                rhs_scale=x_s[:],
                start=True,
                stop=True,
            )

        e00 = psum.tile([P, 256], F32, name="e00", tag="bank0")
        e01 = psum.tile([P, 256], F32, name="e01", tag="bank1")
        e10 = psum.tile([P, 256], F32, name="e10", tag="bank2")
        e11 = psum.tile([P, 256], F32, name="e11", tag="bank3")
        e2 = psum.tile([P, S], F32, name="e2", tag="bank4")
        gate(0, 0, e00[:])
        gate(1, 0, e10[:])
        gate(2, 0, e2[:, 0:256])
        gate(0, 1, e01[:])
        gate(1, 1, e11[:])
        gate(2, 1, e2[:, 256:512])
        nc.scalar.activation(out=sils[0][:, 0:256], in_=e00[:], func=SILU)
        nc.scalar.activation(out=sils[1][:, 0:256], in_=e10[:], func=SILU)
        nc.scalar.activation(out=sils[0][:, 256:512], in_=e01[:], func=SILU)
        nc.scalar.activation(out=sils[1][:, 256:512], in_=e11[:], func=SILU)
        nc.scalar.activation(out=sils[2][:], in_=e2[:], func=SILU)
        up(0, "bank0")
        up(1, "bank1")
        up(2, "bank2")
        e3 = psum.tile([P, S], F32, name="e3", tag="bank3")
        gate(3, 0, e3[:, 0:256])
        gate(3, 1, e3[:, 256:512])
        nc.scalar.activation(out=sils[3][:], in_=e3[:], func=SILU)
        up(3, "bank4")
        for i in range(NT):
            y = held.tile([P, S], F32, name=f"y{i}")
            nc.vector.tensor_tensor(out=y[:], in0=us[i][:], in1=sils[i][:], op=MULT)
            o = held.tile([P, S], F32, name=f"o{i}")
            eng, queue = (nc.gpsimd, nc.scalar) if i < 2 else (nc.vector, nc.sync)
            parts = 2 if i == NT - 1 else 1
            for k in range(parts):
                d = slice(S // parts * k, S // parts * k + S // parts)
                eng.tensor_tensor(out=o[:, d], in0=y[:, d], in1=rts[i][:, d], op=ADD)
                queue.dma_start(out=out[P * i : P * i + P, d], in_=o[:, d])
